import numpy as np
import ml_dtypes


def mxq(x, axis, fmt="e4m3"):
    dtype, down = {"e4m3": (ml_dtypes.float8_e4m3fn, 7), "e5m2": (ml_dtypes.float8_e5m2, 14)}[fmt]
    v = np.moveaxis(np.asarray(x, np.float32).astype(ml_dtypes.bfloat16).astype(np.float64), axis, -1)
    blocks = v.reshape(v.shape[:-1] + (-1, 32))
    amax = np.abs(blocks).max(-1, keepdims=True)
    byte = np.maximum(np.where(amax > 0, np.frexp(amax)[1] - 1 + 127, 0) - down, 1)
    scale = np.exp2(byte - 127.0)
    codes = (blocks / scale).astype(np.float32).astype(dtype).astype(np.float64)
    return np.moveaxis((codes * scale).reshape(v.shape), -1, axis)


WIDE = False


def mx_kscale(k):
    if not WIDE:
        return np.ones(k)
    levels = np.array([10, -10, 5, -5, 0])
    if k % 512:
        return np.exp2(np.random.permutation(np.resize(levels, k // 32))).repeat(32)
    a = np.empty((k // 512, 16))
    for p in range(k // 512):
        a[p, :8] = np.random.permutation(np.resize(levels, 8))
        for g in range(8):
            far = levels[np.abs(levels - a[p, g]) >= 10]
            a[p, g + 8] = far[np.random.randint(len(far))]
    return np.exp2(a.ravel()).repeat(32)


def f64(x):
    return np.asarray(x).astype(np.float64)


def striped(idx):
    return np.tile(idx.reshape(-1, 16).T, (8, 1)).astype(np.uint16)


def unstriped(offs):
    return offs[:16].T.reshape(-1).astype(np.int64)


E2M1 = np.array([0.0, 0.5, 1.0, 1.5, 2.0, 3.0, 4.0, 6.0, -0.0, -0.5, -1.0, -1.5, -2.0, -3.0, -4.0, -6.0])


def pack_fp4(w):
    k, n = w.shape
    w = f64(np.asarray(w, np.float32).astype(ml_dtypes.bfloat16)).reshape(k // 32, 32, n)
    amax = np.abs(w).max(1)
    mant, ex = np.frexp(amax / 6.0)
    byte = np.clip(np.where(amax > 0, np.where(mant > 0.5, ex, ex - 1) + 127, 1), 1, 254)
    scaled = (w * np.exp2(127.0 - byte)[:, None, :]).reshape(k, n).astype(np.float32)
    c = np.ascontiguousarray(scaled.reshape(k // 512, 128, 4, n).transpose(0, 1, 3, 2)).astype(ml_dtypes.float4_e2m1fn).view(np.uint8) & 0xF
    words = (c[..., 0::2] | (c[..., 1::2] << 4)).reshape(k // 512, 128, 2 * n)
    return np.ascontiguousarray(words), np.ascontiguousarray(byte.astype(np.uint8).reshape(k // 512, 16, n))


def unpack_fp4(words, scales):
    g, _, n = scales.shape
    words = np.ascontiguousarray(words).reshape(g, 128, n, 2)
    nib = np.empty((g, 128, n, 4), np.uint8)
    nib[..., 0::2] = words & 0xF
    nib[..., 1::2] = words >> 4
    vals = E2M1[nib] * np.repeat(np.exp2(scales.astype(np.float64) - 127.0), 8, axis=1)[..., None]
    return vals.transpose(0, 1, 3, 2).reshape(g * 512, n)


def relu(v):
    return np.maximum(v, 0.0)


K, T, S, N = 1024, 1024, 512, 256


def setup_inputs():
    n = np.random.standard_normal
    s = mx_kscale(K)[:, None]
    packed_xT = pack_fp4(n((K, T)) * s)
    return {
        "x_words": packed_xT[0],
        "x_scales": packed_xT[1],
        "w1": (n((K, N)) / np.sqrt(3 * K) / s).astype(np.float32),
        "w2": (n((K, N)) / np.sqrt(3 * K) / s).astype(np.float32),
        "w3": (n((K, N)) / np.sqrt(3 * K) / s).astype(np.float32),
        "offs": striped(np.random.permutation(T)[:S]),
    }


def reference(x_words, x_scales, w1, w2, w3, offs):
    xq = unpack_fp4(x_words, x_scales)[:, unstriped(offs)]
    y0 = mxq(f64(w1), 0, "e4m3").T @ xq
    y1 = mxq(f64(w2), 0, "e4m3").T @ xq
    y2 = mxq(f64(w3), 0, "e4m3").T @ xq
    return relu(y0 + np.pad(y1, ((0, 0), (1, 0)))[:, :S] + np.pad(y2, ((0, 0), (2, 0)))[:, :S])

@@ -1,0 +1,163 @@
+from contextlib import ExitStack
+
+import concourse.mybir as mybir
+
+K, T, S, M = 1024, 1024, 512, 256
+TAPS = 3
+FLOPS = 2 * TAPS * K * S * M
+
+F32 = mybir.dt.float32
+BF16 = mybir.dt.bfloat16
+I32 = mybir.dt.int32
+U32 = mybir.dt.uint32
+U16 = mybir.dt.uint16
+U8 = mybir.dt.uint8
+FP8X4 = mybir.dt.float8_e4m3fn_x4
+FP4X4 = mybir.dt.float4_e2m1fn_x4
+ACT = mybir.ActivationFunctionType
+
+P = 128
+PACK = 4
+K_PASS = P * PACK
+PASSES = K // K_PASS
+M_TILES = M // P
+RING = 5
+PAD = 64
+
+
+def tile_picked_listconv_relu_p_kernel(tc, x_words, x_scales, w1, w2, w3, offs, out):
+    nc = tc.nc
+    weights = (w1, w2, w3)
+    with ExitStack() as ctx:
+        keep = ctx.enter_context(tc.tile_pool(name="keep", bufs=1))
+        ring = ctx.enter_context(tc.tile_pool(name="ring", bufs=RING))
+        psum = ctx.enter_context(tc.psum_pool(name="psum", bufs=1))
+
+        offsets = keep.tile([P, S // 16], U16, name="offsets")
+        nc.sync.dma_start(offsets[:], offs)
+
+        scale_table = keep.tile([P, T], U8, name="scale_table", align_bytes=64)
+        nc.vector.memset(scale_table[:].bitcast(I32), 0)
+
+        word_table = [keep.tile([P, T], U16, name=f"word_table{z}", align_bytes=64) for z in range(PASSES)]
+        picked_scales = keep.tile([P, PAD + S], U8, name="picked_scales", align_bytes=64)
+        nc.vector.memset(picked_scales[:, :PAD].bitcast(I32), 0)
+        scales = [keep.tile([P, TAPS * S], U8, name=f"scales{z}", align_bytes=64) for z in range(PASSES)]
+        nc.vector.memset(scales[1][:].bitcast(I32), 0)
+        picked_words, words = {}, {}
+
+        def clear_pad(z, tag):
+            picked_words[z] = keep.tile([P, PAD + 2 * S], U8, name=f"picked_words{z}", tag=tag, align_bytes=64)
+            nc.vector.memset(picked_words[z][:, :PAD].bitcast(I32), 0)
+
+        clear_pad(0, "picked_words0")
+
+        def load_words(z):
+            nc.sync.dma_start(word_table[z][:].bitcast(I32), x_words[z].bitcast(I32))
+
+        def load_scales():
+            for q in range(4):
+                nc.sync.dma_start(
+                    scale_table[32 * q : 32 * q + 8, :].bitcast(I32),
+                    x_scales[:, 4 * q : 4 * q + 4, :].bitcast(I32),
+                )
+
+        chunks = [(z, d) for z in range(PASSES) for d in range(TAPS)]
+        pieces = [(c, 0, M) for c in range(len(chunks) - 1)] + [(len(chunks) - 1, P * t, P) for t in range(M_TILES)]
+        raw_chunks, raw = {}, {}
+        grouped, w_codes, w_scales = [], [], []
+        for i, (c, m0, width) in enumerate(pieces):
+            grouped.append(keep.tile([P, width * PACK], BF16, name=f"grouped{i}", tag=f"grouped{i}", align_bytes=64))
+            w_codes.append(keep.tile([P, width], U32, name=f"w_codes{i}", align_bytes=64))
+            w_scales.append(keep.tile([P, width], U8, name=f"w_scales{i}", align_bytes=64))
+
+        def load_weights(i):
+            c, m0, width = pieces[i]
+            z, d = chunks[c]
+            if m0 == 0:
+                raw_chunks[c] = ring.tile([P, PACK * M], F32, name="raw_chunk", align_bytes=64)
+            raw[i] = raw_chunks[c][:, PACK * m0 : PACK * (m0 + width)].rearrange("p (j m) -> p j m", j=PACK)
+            rows = weights[d][z * K_PASS : (z + 1) * K_PASS, m0 : m0 + width]
+            nc.sync.dma_start(raw[i], rows.rearrange("(p j) m -> p j m", j=PACK))
+
+        def cast(i, on_vector):
+            dst = grouped[i][:].rearrange("p (c i j) -> p c j i", i=4, j=PACK)
+            src = raw[i].rearrange("p j (c i) -> p c j i", i=4)
+            if on_vector:
+                nc.vector.tensor_copy(dst, src)
+            else:
+                nc.scalar.activation(dst, src, ACT.Copy)
+
+        def quantize(i):
+            nc.vector.quantize_mx(out=w_codes[i][:].bitcast(FP8X4), scales=w_scales[i][:], in_=grouped[i][:])
+
+        def gather_scales():
+            nc.vector.tensor_copy(picked_scales[:, PAD:], scale_table[:].indirect(offsets[:]))
+            nc.vector.tensor_copy(scales[0][:, :S].bitcast(I32), picked_scales[:, PAD:].bitcast(I32))
+            for d in range(1, TAPS):
+                nc.vector.tensor_copy(scales[0][:, d * S : (d + 1) * S], picked_scales[:, PAD - d : PAD - d + S])
+            for q in range(4):
+                nc.sync.dma_start(
+                    scales[1][32 * q : 32 * q + 4, :].bitcast(I32),
+                    scales[0][32 * q + 4 : 32 * q + 8, :].bitcast(I32),
+                )
+
+        def gather_words(z):
+            nc.vector.tensor_copy(picked_words[z][:, PAD:].bitcast(U16), word_table[z][:].indirect(offsets[:]))
+            words[z, 0] = picked_words[z][:, PAD:]
+
+        def shift_words(z, d, tag):
+            dtype = I32 if d % 2 == 0 else U8
+            shifted = keep.tile([P, 2 * S], U8, name=f"words{z}_{d}", tag=tag, align_bytes=64)
+            nc.vector.tensor_copy(shifted[:].bitcast(dtype), picked_words[z][:, PAD - 2 * d : PAD + 2 * (S - d)].bitcast(dtype))
+            words[z, d] = shifted[:]
+
+        acc = [psum.tile([P, S], F32, name=f"acc{t}") for t in range(M_TILES)]
+
+        def multiply(i):
+            c, m0, width = pieces[i]
+            z, d = chunks[c]
+            for c0 in range(0, width, P):
+                nc.tensor.matmul_mx(
+                    out=acc[(m0 + c0) // P][:],
+                    lhsT=w_codes[i][:, c0 : c0 + P].bitcast(FP8X4),
+                    lhsT_scale=w_scales[i][:, c0 : c0 + P],
+                    rhs=words[z, d].bitcast(FP4X4),
+                    rhs_scale=scales[z][:, d * S : (d + 1) * S],
+                    start=(c == 0),
+                    stop=(c == len(chunks) - 1),
+                )
+
+        load_words(0)
+        load_weights(0)
+        load_scales()
+        load_weights(1)
+        load_weights(2)
+        load_words(1)
+        load_weights(3)
+        load_weights(4)
+        gather_words(0)
+        gather_scales()
+        for i, (c, m0, width) in enumerate(pieces):
+            z, d = chunks[c]
+            if d == 0 and z > 0:
+                clear_pad(z, f"grouped{i - 1}")
+                gather_words(z)
+            if d > 0 and m0 == 0:
+                shift_words(z, d, f"grouped{i - 1}")
+            cast(i, on_vector=(i == len(pieces) - 2))
+            if c + RING < len(chunks):
+                for n in range(len(pieces)):
+                    if pieces[n][0] == c + RING:
+                        load_weights(n)
+            quantize(i)
+            multiply(i)
+
+        for t in range(M_TILES):
+            result = keep.tile([P, S], F32, name=f"result{t}")
+            if t == 0:
+                nc.scalar.activation(result[:], acc[t][:], ACT.Relu)
+            else:
+                nc.vector.tensor_scalar_max(result[:], acc[t][:], 0.0)
+            queue = nc.scalar if t == 0 else nc.sync
+            queue.dma_start(out[t * P : (t + 1) * P, :], result[:])

@@ -21,8 +21,9 @@ PACK = 4
 K_PASS = P * PACK
 PASSES = K // K_PASS
 M_TILES = M // P
-RING = 5
+RAW_BYTES = PACK * M * 4
 PAD = 64
+N = 128
 
 
 def tile_picked_listconv_relu_p_kernel(tc, x_words, x_scales, w1, w2, w3, offs, out):
@@ -30,27 +31,26 @@ def tile_picked_listconv_relu_p_kernel(tc, x_words, x_scales, w1, w2, w3, offs, 
     weights = (w1, w2, w3)
     with ExitStack() as ctx:
         keep = ctx.enter_context(tc.tile_pool(name="keep", bufs=1))
-        ring = ctx.enter_context(tc.tile_pool(name="ring", bufs=RING))
+        staged = ctx.enter_context(tc.tile_pool(name="staged", bufs=1))
         psum = ctx.enter_context(tc.psum_pool(name="psum", bufs=1))
 
         offsets = keep.tile([P, S // 16], U16, name="offsets")
-        nc.sync.dma_start(offsets[:], offs)
 
         scale_table = keep.tile([P, T], U8, name="scale_table", align_bytes=64)
         nc.vector.memset(scale_table[:].bitcast(I32), 0)
 
         word_table = [keep.tile([P, T], U16, name=f"word_table{z}", align_bytes=64) for z in range(PASSES)]
-        picked_scales = keep.tile([P, PAD + S], U8, name="picked_scales", align_bytes=64)
+        picked_scales = staged.tile([P, PAD + S], U8, name="picked_scales", align_bytes=64, offset=5 * RAW_BYTES)
         nc.vector.memset(picked_scales[:, :PAD].bitcast(I32), 0)
-        scales = [keep.tile([P, TAPS * S], U8, name=f"scales{z}", align_bytes=64) for z in range(PASSES)]
+        scales = {1: keep.tile([P, TAPS * S], U8, name="scales1", align_bytes=64)}
         nc.vector.memset(scales[1][:].bitcast(I32), 0)
         picked_words, words = {}, {}
 
-        def clear_pad(z, tag):
-            picked_words[z] = keep.tile([P, PAD + 2 * S], U8, name=f"picked_words{z}", tag=tag, align_bytes=64)
+        def clear_pad(z, slot):
+            picked_words[z] = staged.tile([P, PAD + 2 * S], U8, name=f"picked_words{z}", align_bytes=64, offset=slot * RAW_BYTES)
             nc.vector.memset(picked_words[z][:, :PAD].bitcast(I32), 0)
 
-        clear_pad(0, "picked_words0")
+        clear_pad(0, 6)
 
         def load_words(z):
             nc.sync.dma_start(word_table[z][:].bitcast(I32), x_words[z].bitcast(I32))
@@ -64,25 +64,23 @@ def tile_picked_listconv_relu_p_kernel(tc, x_words, x_scales, w1, w2, w3, offs, 
 
         chunks = [(z, d) for z in range(PASSES) for d in range(TAPS)]
         pieces = [(c, 0, M) for c in range(len(chunks) - 1)] + [(len(chunks) - 1, P * t, P) for t in range(M_TILES)]
-        raw_chunks, raw = {}, {}
+        raw = {}
         grouped, w_codes, w_scales = [], [], []
         for i, (c, m0, width) in enumerate(pieces):
-            grouped.append(keep.tile([P, width * PACK], BF16, name=f"grouped{i}", tag=f"grouped{i}", align_bytes=64))
+            grouped.append(keep.tile([P, width * PACK], BF16, name=f"grouped{i}", align_bytes=64))
             w_codes.append(keep.tile([P, width], U32, name=f"w_codes{i}", align_bytes=64))
             w_scales.append(keep.tile([P, width], U8, name=f"w_scales{i}", align_bytes=64))
 
-        def load_weights(i):
-            c, m0, width = pieces[i]
+        def load_weights(c):
             z, d = chunks[c]
-            if m0 == 0:
-                raw_chunks[c] = ring.tile([P, PACK * M], F32, name="raw_chunk", align_bytes=64)
-            raw[i] = raw_chunks[c][:, PACK * m0 : PACK * (m0 + width)].rearrange("p (j m) -> p j m", j=PACK)
-            rows = weights[d][z * K_PASS : (z + 1) * K_PASS, m0 : m0 + width]
-            nc.sync.dma_start(raw[i], rows.rearrange("(p j) m -> p j m", j=PACK))
+            raw[c] = staged.tile([P, PACK, M], F32, name=f"raw{c}", align_bytes=64, offset=c * RAW_BYTES)
+            rows = weights[d][z * K_PASS : (z + 1) * K_PASS, :]
+            nc.sync.dma_start(raw[c][:], rows.rearrange("(p j) m -> p j m", j=PACK))
 
         def cast(i, on_vector):
             dst = grouped[i][:].rearrange("p (c i j) -> p c j i", i=4, j=PACK)
-            src = raw[i].rearrange("p j (c i) -> p c j i", i=4)
+            c, m0, width = pieces[i]
+            src = raw[c][:, :, m0 : m0 + width].rearrange("p j (c i) -> p c j i", i=4)
             if on_vector:
                 nc.vector.tensor_copy(dst, src)
             else:
@@ -93,6 +91,9 @@ def tile_picked_listconv_relu_p_kernel(tc, x_words, x_scales, w1, w2, w3, offs, 
 
         def gather_scales():
             nc.vector.tensor_copy(picked_scales[:, PAD:], scale_table[:].indirect(offsets[:]))
+
+        def shift_scales():
+            scales[0] = staged.tile([P, TAPS * S], U8, name="scales0", align_bytes=64, offset=RAW_BYTES // 2)
             nc.vector.tensor_copy(scales[0][:, :S].bitcast(I32), picked_scales[:, PAD:].bitcast(I32))
             for d in range(1, TAPS):
                 nc.vector.tensor_copy(scales[0][:, d * S : (d + 1) * S], picked_scales[:, PAD - d : PAD - d + S])
@@ -106,29 +107,32 @@ def tile_picked_listconv_relu_p_kernel(tc, x_words, x_scales, w1, w2, w3, offs, 
             nc.vector.tensor_copy(picked_words[z][:, PAD:].bitcast(U16), word_table[z][:].indirect(offsets[:]))
             words[z, 0] = picked_words[z][:, PAD:]
 
-        def shift_words(z, d, tag):
-            dtype = I32 if d % 2 == 0 else U8
-            shifted = keep.tile([P, 2 * S], U8, name=f"words{z}_{d}", tag=tag, align_bytes=64)
-            nc.vector.tensor_copy(shifted[:].bitcast(dtype), picked_words[z][:, PAD - 2 * d : PAD + 2 * (S - d)].bitcast(dtype))
-            words[z, d] = shifted[:]
+        def shift_words(z, slot):
+            shifted = staged.tile([P, (TAPS - 1) * 2 * S], U8, name=f"shifted_words{z}", align_bytes=64, offset=slot * RAW_BYTES)
+            for d in range(1, TAPS):
+                dtype = I32 if d % 2 == 0 else U8
+                words[z, d] = shifted[:, (d - 1) * 2 * S : d * 2 * S]
+                nc.vector.tensor_copy(words[z, d].bitcast(dtype), picked_words[z][:, PAD - 2 * d : PAD + 2 * (S - d)].bitcast(dtype))
 
-        acc = [psum.tile([P, S], F32, name=f"acc{t}") for t in range(M_TILES)]
+        acc = [[psum.tile([P, N], F32, name=f"acc{t}_{n}") for n in range(S // N)] for t in range(M_TILES)]
 
         def multiply(i):
             c, m0, width = pieces[i]
             z, d = chunks[c]
             for c0 in range(0, width, P):
-                nc.tensor.matmul_mx(
-                    out=acc[(m0 + c0) // P][:],
-                    lhsT=w_codes[i][:, c0 : c0 + P].bitcast(FP8X4),
-                    lhsT_scale=w_scales[i][:, c0 : c0 + P],
-                    rhs=words[z, d].bitcast(FP4X4),
-                    rhs_scale=scales[z][:, d * S : (d + 1) * S],
-                    start=(c == 0),
-                    stop=(c == len(chunks) - 1),
-                )
+                for n in range(S // N):
+                    nc.tensor.matmul_mx(
+                        out=acc[(m0 + c0) // P][n][:],
+                        lhsT=w_codes[i][:, c0 : c0 + P].bitcast(FP8X4),
+                        lhsT_scale=w_scales[i][:, c0 : c0 + P],
+                        rhs=words[z, d][:, 2 * n * N : 2 * (n + 1) * N].bitcast(FP4X4),
+                        rhs_scale=scales[z][:, d * S + n * N : d * S + (n + 1) * N],
+                        start=(c == 0),
+                        stop=(c == len(chunks) - 1),
+                    )
 
         load_words(0)
+        nc.sync.dma_start(offsets[:], offs)
         load_weights(0)
         load_scales()
         load_weights(1)
@@ -138,26 +142,25 @@ def tile_picked_listconv_relu_p_kernel(tc, x_words, x_scales, w1, w2, w3, offs, 
         load_weights(4)
         gather_words(0)
         gather_scales()
-        for i, (c, m0, width) in enumerate(pieces):
-            z, d = chunks[c]
-            if d == 0 and z > 0:
-                clear_pad(z, f"grouped{i - 1}")
-                gather_words(z)
-            if d > 0 and m0 == 0:
-                shift_words(z, d, f"grouped{i - 1}")
-            cast(i, on_vector=(i == len(pieces) - 2))
-            if c + RING < len(chunks):
-                for n in range(len(pieces)):
-                    if pieces[n][0] == c + RING:
-                        load_weights(n)
-            quantize(i)
-            multiply(i)
+        for c, (z, d) in enumerate(chunks):
+            own = [i for i in range(len(pieces)) if pieces[i][0] == c]
+            for i in own:
+                cast(i, on_vector=(i == len(pieces) - 1))
+            for i in own:
+                quantize(i)
+                if c == 0:
+                    shift_scales()
+                    load_weights(len(chunks) - 1)
+                multiply(i)
+            if d == 0:
+                shift_words(z, c)
+            if d == TAPS - 1 and z + 1 < PASSES:
+                clear_pad(z + 1, c)
+                gather_words(z + 1)
 
         for t in range(M_TILES):
-            result = keep.tile([P, S], F32, name=f"result{t}")
-            if t == 0:
-                nc.scalar.activation(result[:], acc[t][:], ACT.Relu)
-            else:
-                nc.vector.tensor_scalar_max(result[:], acc[t][:], 0.0)
-            queue = nc.scalar if t == 0 else nc.sync
-            queue.dma_start(out[t * P : (t + 1) * P, :], result[:])
+            for h in range(S // (2 * N)):
+                result = keep.tile([P, 2 * N], F32, name=f"result{t}_{h}")
+                nc.scalar.activation(result[:, :N], acc[t][2 * h][:], ACT.Relu)
+                nc.vector.tensor_scalar_max(result[:, N:], acc[t][2 * h + 1][:], 0.0)
+                nc.sync.dma_start(out[t * P : (t + 1) * P, 2 * h * N : 2 * (h + 1) * N], result[:])

@@ -56,11 +56,9 @@ def tile_picked_listconv_relu_p_kernel(tc, x_words, x_scales, w1, w2, w3, offs, 
             nc.sync.dma_start(word_table[z][:].bitcast(I32), x_words[z].bitcast(I32))
 
         def load_scales():
-            for q in range(4):
-                nc.sync.dma_start(
-                    scale_table[32 * q : 32 * q + 8, :].bitcast(I32),
-                    x_scales[:, 4 * q : 4 * q + 4, :].bitcast(I32),
-                )
+            rows = x_scales.rearrange("z (q r) c -> r q z c", r=4)
+            for r in range(4):
+                nc.sync.dma_start(scale_table[r:P:16, :].bitcast(I32), rows[r].bitcast(I32))
 
         chunks = [(z, d) for z in range(PASSES) for d in range(TAPS)]
         pieces = [(c, 0, M) for c in range(len(chunks) - 1)] + [(len(chunks) - 1, P * t, P) for t in range(M_TILES)]
@@ -78,9 +76,9 @@ def tile_picked_listconv_relu_p_kernel(tc, x_words, x_scales, w1, w2, w3, offs, 
             nc.sync.dma_start(raw[c][:], rows.rearrange("(p j) m -> p j m", j=PACK))
 
         def cast(i, on_vector):
-            dst = grouped[i][:].rearrange("p (c i j) -> p c j i", i=4, j=PACK)
+            dst = grouped[i][:].rearrange("p (c i j) -> p c j i", i=2, j=PACK)
             c, m0, width = pieces[i]
-            src = raw[c][:, :, m0 : m0 + width].rearrange("p j (c i) -> p c j i", i=4)
+            src = raw[c][:, :, m0 : m0 + width].rearrange("p j (c i) -> p c j i", i=2)
             if on_vector:
                 nc.vector.tensor_copy(dst, src)
             else:
@@ -100,7 +98,7 @@ def tile_picked_listconv_relu_p_kernel(tc, x_words, x_scales, w1, w2, w3, offs, 
             for q in range(4):
                 nc.sync.dma_start(
                     scales[1][32 * q : 32 * q + 4, :].bitcast(I32),
-                    scales[0][32 * q + 4 : 32 * q + 8, :].bitcast(I32),
+                    scales[0][32 * q + 16 : 32 * q + 20, :].bitcast(I32),
                 )
 
         def gather_words(z):

@@ -24,6 +24,7 @@ M_TILES = M // P
 RAW_BYTES = PACK * M * 4
 PAD = 64
 N = 128
+VECTOR_COLUMNS = 96
 
 
 def tile_picked_listconv_relu_p_kernel(tc, x_words, x_scales, w1, w2, w3, offs, out):
@@ -61,7 +62,8 @@ def tile_picked_listconv_relu_p_kernel(tc, x_words, x_scales, w1, w2, w3, offs, 
                 nc.sync.dma_start(scale_table[r:P:16, :].bitcast(I32), rows[r].bitcast(I32))
 
         chunks = [(z, d) for z in range(PASSES) for d in range(TAPS)]
-        pieces = [(c, 0, M) for c in range(len(chunks) - 1)] + [(len(chunks) - 1, P * t, P) for t in range(M_TILES)]
+        pieces = [(c, 0, M) for c in range(len(chunks) - 2)]
+        pieces = pieces + [(c, P * t, P) for c in range(len(chunks) - 2, len(chunks)) for t in range(M_TILES)]
         raw = {}
         grouped, w_codes, w_scales = [], [], []
         for i, (c, m0, width) in enumerate(pieces):
@@ -75,10 +77,10 @@ def tile_picked_listconv_relu_p_kernel(tc, x_words, x_scales, w1, w2, w3, offs, 
             rows = weights[d][z * K_PASS : (z + 1) * K_PASS, :]
             nc.sync.dma_start(raw[c][:], rows.rearrange("(p j) m -> p j m", j=PACK))
 
-        def cast(i, on_vector):
-            dst = grouped[i][:].rearrange("p (c i j) -> p c j i", i=2, j=PACK)
+        def cast(i, first, last, on_vector):
+            dst = grouped[i][:, PACK * first : PACK * last].rearrange("p (c i j) -> p c j i", i=2, j=PACK)
             c, m0, width = pieces[i]
-            src = raw[c][:, :, m0 : m0 + width].rearrange("p j (c i) -> p c j i", i=2)
+            src = raw[c][:, :, m0 + first : m0 + last].rearrange("p j (c i) -> p c j i", i=2)
             if on_vector:
                 nc.vector.tensor_copy(dst, src)
             else:
@@ -143,7 +145,11 @@ def tile_picked_listconv_relu_p_kernel(tc, x_words, x_scales, w1, w2, w3, offs, 
         for c, (z, d) in enumerate(chunks):
             own = [i for i in range(len(pieces)) if pieces[i][0] == c]
             for i in own:
-                cast(i, on_vector=(i == len(pieces) - 1))
+                if i == len(pieces) - 2:
+                    cast(i, 0, VECTOR_COLUMNS, on_vector=True)
+                    cast(i, VECTOR_COLUMNS, P, on_vector=False)
+                else:
+                    cast(i, 0, pieces[i][2], on_vector=False)
             for i in own:
                 quantize(i)
                 if c == 0:

@@ -47,11 +47,9 @@ def tile_picked_listconv_relu_p_kernel(tc, x_words, x_scales, w1, w2, w3, offs, 
         nc.vector.memset(scales[1][:].bitcast(I32), 0)
         picked_words, words = {}, {}
 
-        def clear_pad(z, slot):
-            picked_words[z] = staged.tile([P, PAD + 2 * S], U8, name=f"picked_words{z}", align_bytes=64, offset=slot * RAW_BYTES)
+        for z in range(PASSES):
+            picked_words[z] = keep.tile([P, PAD + 2 * S], U8, name=f"picked_words{z}", align_bytes=64)
             nc.vector.memset(picked_words[z][:, :PAD].bitcast(I32), 0)
-
-        clear_pad(0, 6)
 
         def load_words(z):
             nc.sync.dma_start(word_table[z][:].bitcast(I32), x_words[z].bitcast(I32))
@@ -156,11 +154,12 @@ def tile_picked_listconv_relu_p_kernel(tc, x_words, x_scales, w1, w2, w3, offs, 
                     shift_scales()
                     load_weights(len(chunks) - 1)
                 multiply(i)
-            if d == 0:
-                shift_words(z, c)
-            if d == TAPS - 1 and z + 1 < PASSES:
-                clear_pad(z + 1, c)
-                gather_words(z + 1)
+            if c == 0:
+                shift_words(0, c)
+            if c == 1:
+                gather_words(1)
+            if c == 2:
+                shift_words(1, c)
 
         for t in range(M_TILES):
             for h in range(S // (2 * N)):

@@ -24,7 +24,8 @@ M_TILES = M // P
 RAW_BYTES = PACK * M * 4
 PAD = 64
 N = 128
-VECTOR_COLUMNS = 96
+FIRST_TILE_VECTOR_COLUMNS = 88
+LAST_TILE_VECTOR_COLUMNS = 64
 
 
 def tile_picked_listconv_relu_p_kernel(tc, x_words, x_scales, w1, w2, w3, offs, out):
@@ -94,7 +95,8 @@ def tile_picked_listconv_relu_p_kernel(tc, x_words, x_scales, w1, w2, w3, offs, 
             scales[0] = staged.tile([P, TAPS * S], U8, name="scales0", align_bytes=64, offset=RAW_BYTES // 2)
             nc.vector.tensor_copy(scales[0][:, :S].bitcast(I32), picked_scales[:, PAD:].bitcast(I32))
             for d in range(1, TAPS):
-                nc.vector.tensor_copy(scales[0][:, d * S : (d + 1) * S], picked_scales[:, PAD - d : PAD - d + S])
+                dtype = U16 if d % 2 == 0 else U8
+                nc.vector.tensor_copy(scales[0][:, d * S : (d + 1) * S].bitcast(dtype), picked_scales[:, PAD - d : PAD - d + S].bitcast(dtype))
             for q in range(4):
                 nc.sync.dma_start(
                     scales[1][32 * q : 32 * q + 4, :].bitcast(I32),
@@ -108,7 +110,7 @@ def tile_picked_listconv_relu_p_kernel(tc, x_words, x_scales, w1, w2, w3, offs, 
         def shift_words(z, slot):
             shifted = staged.tile([P, (TAPS - 1) * 2 * S], U8, name=f"shifted_words{z}", align_bytes=64, offset=slot * RAW_BYTES)
             for d in range(1, TAPS):
-                dtype = I32 if d % 2 == 0 else U8
+                dtype = I32 if d % 2 == 0 else U16
                 words[z, d] = shifted[:, (d - 1) * 2 * S : d * 2 * S]
                 nc.vector.tensor_copy(words[z, d].bitcast(dtype), picked_words[z][:, PAD - 2 * d : PAD + 2 * (S - d)].bitcast(dtype))
 
@@ -129,6 +131,9 @@ def tile_picked_listconv_relu_p_kernel(tc, x_words, x_scales, w1, w2, w3, offs, 
                         stop=(c == len(chunks) - 1),
                     )
 
+        last = len(pieces) - 1
+        vector_columns = {last - 3: P, last - 1: FIRST_TILE_VECTOR_COLUMNS, last: LAST_TILE_VECTOR_COLUMNS}
+
         load_words(0)
         nc.sync.dma_start(offsets[:], offs)
         load_weights(0)
@@ -143,11 +148,11 @@ def tile_picked_listconv_relu_p_kernel(tc, x_words, x_scales, w1, w2, w3, offs, 
         for c, (z, d) in enumerate(chunks):
             own = [i for i in range(len(pieces)) if pieces[i][0] == c]
             for i in own:
-                if i == len(pieces) - 2:
-                    cast(i, 0, VECTOR_COLUMNS, on_vector=True)
-                    cast(i, VECTOR_COLUMNS, P, on_vector=False)
-                else:
-                    cast(i, 0, pieces[i][2], on_vector=False)
+                share = vector_columns.get(i, 0)
+                if share > 0:
+                    cast(i, 0, share, on_vector=True)
+                if share < pieces[i][2]:
+                    cast(i, share, pieces[i][2], on_vector=False)
             for i in own:
                 quantize(i)
                 if c == 0:

@@ -24,8 +24,7 @@ M_TILES = M // P
 RAW_BYTES = PACK * M * 4
 PAD = 64
 N = 128
-FIRST_TILE_VECTOR_COLUMNS = 88
-LAST_TILE_VECTOR_COLUMNS = 64
+VECTOR_COLUMNS = 88
 
 
 def tile_picked_listconv_relu_p_kernel(tc, x_words, x_scales, w1, w2, w3, offs, out):
@@ -42,7 +41,7 @@ def tile_picked_listconv_relu_p_kernel(tc, x_words, x_scales, w1, w2, w3, offs, 
         nc.vector.memset(scale_table[:].bitcast(I32), 0)
 
         word_table = [keep.tile([P, T], U16, name=f"word_table{z}", align_bytes=64) for z in range(PASSES)]
-        picked_scales = staged.tile([P, PAD + S], U8, name="picked_scales", align_bytes=64, offset=5 * RAW_BYTES)
+        picked_scales = staged.tile([P, PAD + S], U8, name="picked_scales", align_bytes=64, offset=5 * RAW_BYTES + RAW_BYTES // 2 - 4 * PAD)
         nc.vector.memset(picked_scales[:, :PAD].bitcast(I32), 0)
         scales = {1: keep.tile([P, TAPS * S], U8, name="scales1", align_bytes=64)}
         nc.vector.memset(scales[1][:].bitcast(I32), 0)
@@ -72,14 +71,19 @@ def tile_picked_listconv_relu_p_kernel(tc, x_words, x_scales, w1, w2, w3, offs, 
 
         def load_weights(c):
             z, d = chunks[c]
-            raw[c] = staged.tile([P, PACK, M], F32, name=f"raw{c}", align_bytes=64, offset=c * RAW_BYTES)
-            rows = weights[d][z * K_PASS : (z + 1) * K_PASS, :]
-            nc.sync.dma_start(raw[c][:], rows.rearrange("(p j) m -> p j m", j=PACK))
+            width = P if c == len(chunks) - 1 else M
+            for m0 in range(0, M, width):
+                tile = staged.tile([P, PACK, width], F32, name=f"raw{c}_{m0}", align_bytes=64, offset=c * RAW_BYTES + m0 * PACK * 4)
+                rows = weights[d][z * K_PASS : (z + 1) * K_PASS, m0 : m0 + width]
+                nc.sync.dma_start(tile[:], rows.rearrange("(p j) m -> p j m", j=PACK))
+                for t0 in range(0, width, P):
+                    raw[c, m0 + t0] = (tile, t0)
 
         def cast(i, first, last, on_vector):
             dst = grouped[i][:, PACK * first : PACK * last].rearrange("p (c i j) -> p c j i", i=2, j=PACK)
             c, m0, width = pieces[i]
-            src = raw[c][:, :, m0 + first : m0 + last].rearrange("p j (c i) -> p c j i", i=2)
+            tile, t0 = raw[c, m0]
+            src = tile[:, :, t0 + first : t0 + last].rearrange("p j (c i) -> p c j i", i=2)
             if on_vector:
                 nc.vector.tensor_copy(dst, src)
             else:
@@ -132,7 +136,7 @@ def tile_picked_listconv_relu_p_kernel(tc, x_words, x_scales, w1, w2, w3, offs, 
                     )
 
         last = len(pieces) - 1
-        vector_columns = {last - 3: P, last - 1: FIRST_TILE_VECTOR_COLUMNS, last: LAST_TILE_VECTOR_COLUMNS}
+        vector_columns = {last - 3: P, last - 1: VECTOR_COLUMNS, last: VECTOR_COLUMNS}
 
         load_words(0)
         nc.sync.dma_start(offsets[:], offs)
@@ -168,7 +172,13 @@ def tile_picked_listconv_relu_p_kernel(tc, x_words, x_scales, w1, w2, w3, offs, 
 
         for t in range(M_TILES):
             for h in range(S // (2 * N)):
-                result = keep.tile([P, 2 * N], F32, name=f"result{t}_{h}")
-                nc.scalar.activation(result[:, :N], acc[t][2 * h][:], ACT.Relu)
-                nc.vector.tensor_scalar_max(result[:, N:], acc[t][2 * h + 1][:], 0.0)
+                if t == 0:
+                    at = 5 * RAW_BYTES + RAW_BYTES // 2 + h * 2 * N * 4
+                    result = staged.tile([P, 2 * N], F32, name=f"result{t}_{h}", align_bytes=64, offset=at)
+                    nc.scalar.activation(result[:, :N], acc[t][2 * h][:], ACT.Relu)
+                    nc.scalar.activation(result[:, N:], acc[t][2 * h + 1][:], ACT.Relu)
+                else:
+                    result = keep.tile([P, 2 * N], F32, name=f"result{t}_{h}")
+                    nc.scalar.activation(result[:, :N], acc[t][2 * h][:], ACT.Relu)
+                    nc.vector.tensor_scalar_max(result[:, N:], acc[t][2 * h + 1][:], 0.0)
                 nc.sync.dma_start(out[t * P : (t + 1) * P, 2 * h * N : 2 * (h + 1) * N], result[:])

@@ -80,10 +80,10 @@ def tile_picked_listconv_relu_p_kernel(tc, x_words, x_scales, w1, w2, w3, offs, 
                     raw[c, m0 + t0] = (tile, t0)
 
         def cast(i, first, last, on_vector):
-            dst = grouped[i][:, PACK * first : PACK * last].rearrange("p (c i j) -> p c j i", i=2, j=PACK)
+            dst = grouped[i][:, PACK * first : PACK * last].rearrange("p (c i j) -> p c j i", i=4, j=PACK)
             c, m0, width = pieces[i]
             tile, t0 = raw[c, m0]
-            src = tile[:, :, t0 + first : t0 + last].rearrange("p j (c i) -> p c j i", i=2)
+            src = tile[:, :, t0 + first : t0 + last].rearrange("p j (c i) -> p c j i", i=4)
             if on_vector:
                 nc.vector.tensor_copy(dst, src)
             else:

@@ -136,7 +136,7 @@ def tile_picked_listconv_relu_p_kernel(tc, x_words, x_scales, w1, w2, w3, offs, 
                     )
 
         last = len(pieces) - 1
-        vector_columns = {last - 3: P, last - 1: VECTOR_COLUMNS, last: VECTOR_COLUMNS}
+        vector_columns = {last - 3: P, last - 1: P, last: VECTOR_COLUMNS}
 
         load_words(0)
         nc.sync.dma_start(offsets[:], offs)
@@ -175,10 +175,8 @@ def tile_picked_listconv_relu_p_kernel(tc, x_words, x_scales, w1, w2, w3, offs, 
                 if t == 0:
                     at = 5 * RAW_BYTES + RAW_BYTES // 2 + h * 2 * N * 4
                     result = staged.tile([P, 2 * N], F32, name=f"result{t}_{h}", align_bytes=64, offset=at)
-                    nc.scalar.activation(result[:, :N], acc[t][2 * h][:], ACT.Relu)
-                    nc.scalar.activation(result[:, N:], acc[t][2 * h + 1][:], ACT.Relu)
                 else:
                     result = keep.tile([P, 2 * N], F32, name=f"result{t}_{h}")
-                    nc.scalar.activation(result[:, :N], acc[t][2 * h][:], ACT.Relu)
-                    nc.vector.tensor_scalar_max(result[:, N:], acc[t][2 * h + 1][:], 0.0)
+                nc.scalar.activation(result[:, :N], acc[t][2 * h][:], ACT.Relu)
+                nc.vector.tensor_scalar_max(result[:, N:], acc[t][2 * h + 1][:], 0.0)
                 nc.sync.dma_start(out[t * P : (t + 1) * P, 2 * h * N : 2 * (h + 1) * N], result[:])

@@ -101,10 +101,10 @@ def tile_picked_listconv_relu_p_kernel(tc, x_words, x_scales, w1, w2, w3, offs, 
             for d in range(1, TAPS):
                 dtype = U16 if d % 2 == 0 else U8
                 nc.vector.tensor_copy(scales[0][:, d * S : (d + 1) * S].bitcast(dtype), picked_scales[:, PAD - d : PAD - d + S].bitcast(dtype))
-            for q in range(4):
+            for r in range(4):
                 nc.sync.dma_start(
-                    scales[1][32 * q : 32 * q + 4, :].bitcast(I32),
-                    scales[0][32 * q + 16 : 32 * q + 20, :].bitcast(I32),
+                    scales[1][r:P:32, :].bitcast(I32),
+                    scales[0][16 + r : P : 32, :].bitcast(I32),
                 )
 
         def gather_words(z):

@@ -24,7 +24,7 @@ M_TILES = M // P
 RAW_BYTES = PACK * M * 4
 PAD = 64
 N = 128
-VECTOR_COLUMNS = 88
+VECTOR_COLUMNS = 64
 
 
 def tile_picked_listconv_relu_p_kernel(tc, x_words, x_scales, w1, w2, w3, offs, out):
@@ -69,11 +69,12 @@ def tile_picked_listconv_relu_p_kernel(tc, x_words, x_scales, w1, w2, w3, offs, 
             w_codes.append(keep.tile([P, width], U32, name=f"w_codes{i}", align_bytes=64))
             w_scales.append(keep.tile([P, width], U8, name=f"w_scales{i}", align_bytes=64))
 
-        def load_weights(c):
+        def load_weights(c, starts=(0,)):
             z, d = chunks[c]
             width = P if c == len(chunks) - 1 else M
-            for m0 in range(0, M, width):
-                tile = staged.tile([P, PACK, width], F32, name=f"raw{c}_{m0}", align_bytes=64, offset=c * RAW_BYTES + m0 * PACK * 4)
+            for m0 in starts:
+                at = {(4, 0): 4 * RAW_BYTES + RAW_BYTES // 2, (5, 0): 4 * RAW_BYTES}.get((c, m0), c * RAW_BYTES + m0 * PACK * 4)
+                tile = staged.tile([P, PACK, width], F32, name=f"raw{c}_{m0}", align_bytes=64, offset=at)
                 rows = weights[d][z * K_PASS : (z + 1) * K_PASS, m0 : m0 + width]
                 nc.sync.dma_start(tile[:], rows.rearrange("(p j) m -> p j m", j=PACK))
                 for t0 in range(0, width, P):
@@ -118,25 +119,29 @@ def tile_picked_listconv_relu_p_kernel(tc, x_words, x_scales, w1, w2, w3, offs, 
                 words[z, d] = shifted[:, (d - 1) * 2 * S : d * 2 * S]
                 nc.vector.tensor_copy(words[z, d].bitcast(dtype), picked_words[z][:, PAD - 2 * d : PAD + 2 * (S - d)].bitcast(dtype))
 
-        acc = [[psum.tile([P, N], F32, name=f"acc{t}_{n}") for n in range(S // N)] for t in range(M_TILES)]
+        widths = (2 * N, N)
+        acc = [[psum.tile([P, widths[t]], F32, name=f"acc{t}_{n}") for n in range(S // widths[t])] for t in range(M_TILES)]
 
-        def multiply(i):
+        def multiply(i, starts, stop=False):
             c, m0, width = pieces[i]
             z, d = chunks[c]
-            for c0 in range(0, width, P):
-                for n in range(S // N):
+            for c0 in starts:
+                t = (m0 + c0) // P
+                w = widths[t]
+                for n in range(S // w):
                     nc.tensor.matmul_mx(
-                        out=acc[(m0 + c0) // P][n][:],
+                        out=acc[t][n][:],
                         lhsT=w_codes[i][:, c0 : c0 + P].bitcast(FP8X4),
                         lhsT_scale=w_scales[i][:, c0 : c0 + P],
-                        rhs=words[z, d][:, 2 * n * N : 2 * (n + 1) * N].bitcast(FP4X4),
-                        rhs_scale=scales[z][:, d * S + n * N : d * S + (n + 1) * N],
+                        rhs=words[z, d][:, 2 * n * w : 2 * (n + 1) * w].bitcast(FP4X4),
+                        rhs_scale=scales[z][:, d * S + n * w : d * S + (n + 1) * w],
                         start=(c == 0),
-                        stop=(c == len(chunks) - 1),
+                        stop=stop,
                     )
 
-        last = len(pieces) - 1
-        vector_columns = {last - 3: P, last - 1: P, last: VECTOR_COLUMNS}
+        def cast_shared(i):
+            cast(i, 0, VECTOR_COLUMNS, on_vector=True)
+            cast(i, VECTOR_COLUMNS, P, on_vector=False)
 
         load_words(0)
         nc.sync.dma_start(offsets[:], offs)
@@ -146,29 +151,38 @@ def tile_picked_listconv_relu_p_kernel(tc, x_words, x_scales, w1, w2, w3, offs, 
         load_weights(2)
         load_words(1)
         load_weights(3)
-        load_weights(4)
+        load_weights(5)
         gather_words(0)
         gather_scales()
-        for c, (z, d) in enumerate(chunks):
-            own = [i for i in range(len(pieces)) if pieces[i][0] == c]
-            for i in own:
-                share = vector_columns.get(i, 0)
-                if share > 0:
-                    cast(i, 0, share, on_vector=True)
-                if share < pieces[i][2]:
-                    cast(i, share, pieces[i][2], on_vector=False)
-            for i in own:
-                quantize(i)
-                if c == 0:
-                    shift_scales()
-                    load_weights(len(chunks) - 1)
-                multiply(i)
+        for c in range(TAPS + 1):
+            cast(c, 0, M, on_vector=False)
+            quantize(c)
+            if c == 0:
+                shift_scales()
+                load_weights(4)
+                load_weights(5, starts=(P,))
+            if c < TAPS:
+                multiply(c, (0, P))
             if c == 0:
                 shift_words(0, c)
             if c == 1:
                 gather_words(1)
             if c == 2:
                 shift_words(1, c)
+        cast(6, 0, P, on_vector=True)
+        quantize(6)
+        cast_shared(4)
+        cast_shared(5)
+        quantize(4)
+        quantize(5)
+        cast_shared(7)
+        quantize(7)
+        multiply(3, (0,))
+        multiply(6, (0,))
+        multiply(3, (P,))
+        multiply(4, (0,), stop=True)
+        multiply(5, (0,))
+        multiply(7, (0,), stop=True)
 
         for t in range(M_TILES):
             for h in range(S // (2 * N)):
@@ -177,6 +191,9 @@ def tile_picked_listconv_relu_p_kernel(tc, x_words, x_scales, w1, w2, w3, offs, 
                     result = staged.tile([P, 2 * N], F32, name=f"result{t}_{h}", align_bytes=64, offset=at)
                 else:
                     result = keep.tile([P, 2 * N], F32, name=f"result{t}_{h}")
-                nc.scalar.activation(result[:, :N], acc[t][2 * h][:], ACT.Relu)
-                nc.vector.tensor_scalar_max(result[:, N:], acc[t][2 * h + 1][:], 0.0)
+                if t == 1:
+                    nc.scalar.activation(result[:, :N], acc[t][2 * h][:], ACT.Relu)
+                    nc.vector.tensor_scalar_max(result[:, N:], acc[t][2 * h + 1][:], 0.0)
+                else:
+                    nc.scalar.activation(result[:], acc[t][h][:], ACT.Relu)
                 nc.sync.dma_start(out[t * P : (t + 1) * P, 2 * h * N : 2 * (h + 1) * N], result[:])

@@ -37,14 +37,17 @@ def tile_picked_listconv_relu_p_kernel(tc, x_words, x_scales, w1, w2, w3, offs, 
 
         offsets = keep.tile([P, S // 16], U16, name="offsets")
 
-        scale_table = keep.tile([P, T], U8, name="scale_table", align_bytes=64)
+        scale_table = staged.tile([P, T], U8, name="scale_table", align_bytes=64, offset=4 * RAW_BYTES + RAW_BYTES // 2 - T // 2)
         nc.vector.memset(scale_table[:].bitcast(I32), 0)
 
         word_table = [keep.tile([P, T], U16, name=f"word_table{z}", align_bytes=64) for z in range(PASSES)]
-        picked_scales = staged.tile([P, PAD + S], U8, name="picked_scales", align_bytes=64, offset=5 * RAW_BYTES + RAW_BYTES // 2 - 4 * PAD)
-        nc.vector.memset(picked_scales[:, :PAD].bitcast(I32), 0)
-        scales = {1: keep.tile([P, TAPS * S], U8, name="scales1", align_bytes=64)}
-        nc.vector.memset(scales[1][:].bitcast(I32), 0)
+        picked_scales = [
+            staged.tile([P, PAD + S], U8, name="picked_scales0", align_bytes=64, offset=6 * RAW_BYTES),
+            keep.tile([P, PAD + S], U8, name="picked_scales1", align_bytes=64),
+        ]
+        nc.vector.memset(picked_scales[0][:, :PAD].bitcast(I32), 0)
+        nc.vector.memset(picked_scales[1][:].bitcast(I32), 0)
+        scales = {(z, 0): picked_scales[z][:, PAD:] for z in range(PASSES)}
         picked_words, words = {}, {}
 
         for z in range(PASSES):
@@ -66,7 +69,10 @@ def tile_picked_listconv_relu_p_kernel(tc, x_words, x_scales, w1, w2, w3, offs, 
         grouped, w_codes, w_scales = [], [], []
         for i, (c, m0, width) in enumerate(pieces):
             grouped.append(keep.tile([P, width * PACK], BF16, name=f"grouped{i}", align_bytes=64))
-            w_codes.append(keep.tile([P, width], U32, name=f"w_codes{i}", align_bytes=64))
+            if i == TAPS:
+                w_codes.append(staged.tile([P, width], U32, name=f"w_codes{i}", align_bytes=64, offset=6 * RAW_BYTES))
+            else:
+                w_codes.append(keep.tile([P, width], U32, name=f"w_codes{i}", align_bytes=64))
             w_scales.append(keep.tile([P, width], U8, name=f"w_scales{i}", align_bytes=64))
 
         def load_weights(c, starts=(0,)):
@@ -94,19 +100,19 @@ def tile_picked_listconv_relu_p_kernel(tc, x_words, x_scales, w1, w2, w3, offs, 
             nc.vector.quantize_mx(out=w_codes[i][:].bitcast(FP8X4), scales=w_scales[i][:], in_=grouped[i][:])
 
         def gather_scales():
-            nc.vector.tensor_copy(picked_scales[:, PAD:], scale_table[:].indirect(offsets[:]))
-
-        def shift_scales():
-            scales[0] = staged.tile([P, TAPS * S], U8, name="scales0", align_bytes=64, offset=RAW_BYTES // 2)
-            nc.vector.tensor_copy(scales[0][:, :S].bitcast(I32), picked_scales[:, PAD:].bitcast(I32))
-            for d in range(1, TAPS):
-                dtype = U16 if d % 2 == 0 else U8
-                nc.vector.tensor_copy(scales[0][:, d * S : (d + 1) * S].bitcast(dtype), picked_scales[:, PAD - d : PAD - d + S].bitcast(dtype))
+            nc.vector.tensor_copy(picked_scales[0][:, PAD:], scale_table[:].indirect(offsets[:]))
             for r in range(4):
                 nc.sync.dma_start(
-                    scales[1][r:P:32, :].bitcast(I32),
-                    scales[0][16 + r : P : 32, :].bitcast(I32),
+                    picked_scales[1][r:P:32, PAD:].bitcast(I32),
+                    picked_scales[0][16 + r : P : 32, PAD:].bitcast(I32),
                 )
+
+        def shift_scales(z, slot):
+            shifted = staged.tile([P, (TAPS - 1) * S], U8, name=f"shifted_scales{z}", align_bytes=64, offset=slot * RAW_BYTES + RAW_BYTES // 2)
+            for d in range(1, TAPS):
+                dtype = U16 if d % 2 == 0 else U8
+                scales[z, d] = shifted[:, (d - 1) * S : d * S]
+                nc.vector.tensor_copy(scales[z, d].bitcast(dtype), picked_scales[z][:, PAD - d : PAD - d + S].bitcast(dtype))
 
         def gather_words(z):
             nc.vector.tensor_copy(picked_words[z][:, PAD:].bitcast(U16), word_table[z][:].indirect(offsets[:]))
@@ -134,7 +140,7 @@ def tile_picked_listconv_relu_p_kernel(tc, x_words, x_scales, w1, w2, w3, offs, 
                         lhsT=w_codes[i][:, c0 : c0 + P].bitcast(FP8X4),
                         lhsT_scale=w_scales[i][:, c0 : c0 + P],
                         rhs=words[z, d][:, 2 * n * w : 2 * (n + 1) * w].bitcast(FP4X4),
-                        rhs_scale=scales[z][:, d * S + n * w : d * S + (n + 1) * w],
+                        rhs_scale=scales[z, d][:, n * w : (n + 1) * w],
                         start=(c == 0),
                         stop=stop,
                     )
@@ -151,25 +157,25 @@ def tile_picked_listconv_relu_p_kernel(tc, x_words, x_scales, w1, w2, w3, offs, 
         load_weights(2)
         load_words(1)
         load_weights(3)
-        load_weights(5)
         gather_words(0)
         gather_scales()
+        load_weights(5)
+        load_weights(4)
+        load_weights(5, starts=(P,))
         for c in range(TAPS + 1):
             cast(c, 0, M, on_vector=False)
             quantize(c)
-            if c == 0:
-                shift_scales()
-                load_weights(4)
-                load_weights(5, starts=(P,))
             if c < TAPS:
                 multiply(c, (0, P))
             if c == 0:
                 shift_words(0, c)
+                shift_scales(0, c)
             if c == 1:
                 gather_words(1)
             if c == 2:
                 shift_words(1, c)
-        cast(6, 0, P, on_vector=True)
+                shift_scales(1, c)
+        cast(6, 0, P, on_vector=False)
         quantize(6)
         cast_shared(4)
         cast_shared(5)

@@ -37,7 +37,7 @@ def tile_picked_listconv_relu_p_kernel(tc, x_words, x_scales, w1, w2, w3, offs, 
 
         offsets = keep.tile([P, S // 16], U16, name="offsets")
 
-        scale_table = staged.tile([P, T], U8, name="scale_table", align_bytes=64, offset=4 * RAW_BYTES + RAW_BYTES // 2 - T // 2)
+        scale_table = staged.tile([P, T], U8, name="scale_table", align_bytes=64, offset=5 * RAW_BYTES + RAW_BYTES // 2 - T // 2)
         nc.vector.memset(scale_table[:].bitcast(I32), 0)
 
         word_table = [keep.tile([P, T], U16, name=f"word_table{z}", align_bytes=64) for z in range(PASSES)]
@@ -156,17 +156,16 @@ def tile_picked_listconv_relu_p_kernel(tc, x_words, x_scales, w1, w2, w3, offs, 
         load_weights(1)
         load_weights(2)
         load_words(1)
+        load_weights(5)
         load_weights(3)
         gather_words(0)
         gather_scales()
-        load_weights(5)
         load_weights(4)
         load_weights(5, starts=(P,))
-        for c in range(TAPS + 1):
+        for c in range(TAPS):
             cast(c, 0, M, on_vector=False)
             quantize(c)
-            if c < TAPS:
-                multiply(c, (0, P))
+            multiply(c, (0, P))
             if c == 0:
                 shift_words(0, c)
                 shift_scales(0, c)
@@ -174,17 +173,20 @@ def tile_picked_listconv_relu_p_kernel(tc, x_words, x_scales, w1, w2, w3, offs, 
                 gather_words(1)
             if c == 2:
                 shift_words(1, c)
-                shift_scales(1, c)
         cast(6, 0, P, on_vector=False)
         quantize(6)
+        cast(3, 0, VECTOR_COLUMNS, on_vector=True)
+        cast(3, VECTOR_COLUMNS, M, on_vector=False)
+        shift_scales(1, 2)
+        quantize(3)
         cast_shared(4)
         cast_shared(5)
         quantize(4)
         quantize(5)
         cast_shared(7)
         quantize(7)
-        multiply(3, (0,))
         multiply(6, (0,))
+        multiply(3, (0,))
         multiply(3, (P,))
         multiply(4, (0,), stop=True)
         multiply(5, (0,))
@@ -192,11 +194,7 @@ def tile_picked_listconv_relu_p_kernel(tc, x_words, x_scales, w1, w2, w3, offs, 
 
         for t in range(M_TILES):
             for h in range(S // (2 * N)):
-                if t == 0:
-                    at = 5 * RAW_BYTES + RAW_BYTES // 2 + h * 2 * N * 4
-                    result = staged.tile([P, 2 * N], F32, name=f"result{t}_{h}", align_bytes=64, offset=at)
-                else:
-                    result = keep.tile([P, 2 * N], F32, name=f"result{t}_{h}")
+                result = keep.tile([P, 2 * N], F32, name=f"result{t}_{h}")
                 if t == 1:
                     nc.scalar.activation(result[:, :N], acc[t][2 * h][:], ACT.Relu)
                     nc.vector.tensor_scalar_max(result[:, N:], acc[t][2 * h + 1][:], 0.0)

from contextlib import ExitStack

import concourse.mybir as mybir

K, T, S, M = 1024, 1024, 512, 256
TAPS = 3
FLOPS = 2 * TAPS * K * S * M

F32 = mybir.dt.float32
BF16 = mybir.dt.bfloat16
I32 = mybir.dt.int32
U32 = mybir.dt.uint32
U16 = mybir.dt.uint16
U8 = mybir.dt.uint8
FP8X4 = mybir.dt.float8_e4m3fn_x4
FP4X4 = mybir.dt.float4_e2m1fn_x4
ACT = mybir.ActivationFunctionType

P = 128
PACK = 4
K_PASS = P * PACK
PASSES = K // K_PASS
M_TILES = M // P
RAW_BYTES = PACK * M * 4
PAD = 64
N = 128
VECTOR_COLUMNS = 64


def tile_picked_listconv_relu_p_kernel(tc, x_words, x_scales, w1, w2, w3, offs, out):
    nc = tc.nc
    weights = (w1, w2, w3)
    with ExitStack() as ctx:
        keep = ctx.enter_context(tc.tile_pool(name="keep", bufs=1))
        staged = ctx.enter_context(tc.tile_pool(name="staged", bufs=1))
        psum = ctx.enter_context(tc.psum_pool(name="psum", bufs=1))

        offsets = keep.tile([P, S // 16], U16, name="offsets")

        scale_table = staged.tile([P, T], U8, name="scale_table", align_bytes=64, offset=5 * RAW_BYTES + RAW_BYTES // 2 - T // 2)
        nc.vector.memset(scale_table[:].bitcast(I32), 0)

        word_table = [keep.tile([P, T], U16, name=f"word_table{z}", align_bytes=64) for z in range(PASSES)]
        picked_scales = [
            staged.tile([P, PAD + S], U8, name="picked_scales0", align_bytes=64, offset=6 * RAW_BYTES),
            keep.tile([P, PAD + S], U8, name="picked_scales1", align_bytes=64),
        ]
        nc.vector.memset(picked_scales[0][:, :PAD].bitcast(I32), 0)
        nc.vector.memset(picked_scales[1][:].bitcast(I32), 0)
        scales = {(z, 0): picked_scales[z][:, PAD:] for z in range(PASSES)}
        picked_words, words = {}, {}

        for z in range(PASSES):
            picked_words[z] = keep.tile([P, PAD + 2 * S], U8, name=f"picked_words{z}", align_bytes=64)
            nc.vector.memset(picked_words[z][:, :PAD].bitcast(I32), 0)

        def load_words(z):
            nc.sync.dma_start(word_table[z][:].bitcast(I32), x_words[z].bitcast(I32))

        def load_scales():
            rows = x_scales.rearrange("z (q r) c -> r q z c", r=4)
            for r in range(4):
                nc.sync.dma_start(scale_table[r:P:16, :].bitcast(I32), rows[r].bitcast(I32))

        chunks = [(z, d) for z in range(PASSES) for d in range(TAPS)]
        pieces = [(c, 0, M) for c in range(len(chunks) - 2)]
        pieces = pieces + [(c, P * t, P) for c in range(len(chunks) - 2, len(chunks)) for t in range(M_TILES)]
        raw = {}
        grouped, w_codes, w_scales = [], [], []
        for i, (c, m0, width) in enumerate(pieces):
            grouped.append(keep.tile([P, width * PACK], BF16, name=f"grouped{i}", align_bytes=64))
            if i == TAPS:
                w_codes.append(staged.tile([P, width], U32, name=f"w_codes{i}", align_bytes=64, offset=6 * RAW_BYTES))
            else:
                w_codes.append(keep.tile([P, width], U32, name=f"w_codes{i}", align_bytes=64))
            w_scales.append(keep.tile([P, width], U8, name=f"w_scales{i}", align_bytes=64))

        def load_weights(c, starts=(0,)):
            z, d = chunks[c]
            width = P if c == len(chunks) - 1 else M
            for m0 in starts:
                at = {(4, 0): 4 * RAW_BYTES + RAW_BYTES // 2, (5, 0): 4 * RAW_BYTES}.get((c, m0), c * RAW_BYTES + m0 * PACK * 4)
                tile = staged.tile([P, PACK, width], F32, name=f"raw{c}_{m0}", align_bytes=64, offset=at)
                rows = weights[d][z * K_PASS : (z + 1) * K_PASS, m0 : m0 + width]
                nc.sync.dma_start(tile[:], rows.rearrange("(p j) m -> p j m", j=PACK))
                for t0 in range(0, width, P):
                    raw[c, m0 + t0] = (tile, t0)

        def cast(i, first, last, on_vector):
            dst = grouped[i][:, PACK * first : PACK * last].rearrange("p (c i j) -> p c j i", i=4, j=PACK)
            c, m0, width = pieces[i]
            tile, t0 = raw[c, m0]
            src = tile[:, :, t0 + first : t0 + last].rearrange("p j (c i) -> p c j i", i=4)
            if on_vector:
                nc.vector.tensor_copy(dst, src)
            else:
                nc.scalar.activation(dst, src, ACT.Copy)

        def quantize(i):
            nc.vector.quantize_mx(out=w_codes[i][:].bitcast(FP8X4), scales=w_scales[i][:], in_=grouped[i][:])

        def gather_scales():
            nc.vector.tensor_copy(picked_scales[0][:, PAD:], scale_table[:].indirect(offsets[:]))
            for r in range(4):
                nc.sync.dma_start(
                    picked_scales[1][r:P:32, PAD:].bitcast(I32),
                    picked_scales[0][16 + r : P : 32, PAD:].bitcast(I32),
                )

        def shift_scales(z, slot):
            shifted = staged.tile([P, (TAPS - 1) * S], U8, name=f"shifted_scales{z}", align_bytes=64, offset=slot * RAW_BYTES + RAW_BYTES // 2)
            for d in range(1, TAPS):
                dtype = U16 if d % 2 == 0 else U8
                scales[z, d] = shifted[:, (d - 1) * S : d * S]
                nc.vector.tensor_copy(scales[z, d].bitcast(dtype), picked_scales[z][:, PAD - d : PAD - d + S].bitcast(dtype))

        def gather_words(z):
            nc.vector.tensor_copy(picked_words[z][:, PAD:].bitcast(U16), word_table[z][:].indirect(offsets[:]))
            words[z, 0] = picked_words[z][:, PAD:]

        def shift_words(z, slot):
            shifted = staged.tile([P, (TAPS - 1) * 2 * S], U8, name=f"shifted_words{z}", align_bytes=64, offset=slot * RAW_BYTES)
            for d in range(1, TAPS):
                dtype = I32 if d % 2 == 0 else U16
                words[z, d] = shifted[:, (d - 1) * 2 * S : d * 2 * S]
                nc.vector.tensor_copy(words[z, d].bitcast(dtype), picked_words[z][:, PAD - 2 * d : PAD + 2 * (S - d)].bitcast(dtype))

        widths = (2 * N, N)
        acc = [[psum.tile([P, widths[t]], F32, name=f"acc{t}_{n}") for n in range(S // widths[t])] for t in range(M_TILES)]

        def multiply(i, starts, stop=False):
            c, m0, width = pieces[i]
            z, d = chunks[c]
            for c0 in starts:
                t = (m0 + c0) // P
                w = widths[t]
                for n in range(S // w):
                    nc.tensor.matmul_mx(
                        out=acc[t][n][:],
                        lhsT=w_codes[i][:, c0 : c0 + P].bitcast(FP8X4),
                        lhsT_scale=w_scales[i][:, c0 : c0 + P],
                        rhs=words[z, d][:, 2 * n * w : 2 * (n + 1) * w].bitcast(FP4X4),
                        rhs_scale=scales[z, d][:, n * w : (n + 1) * w],
                        start=(c == 0),
                        stop=stop,
                    )

        def cast_shared(i):
            cast(i, 0, VECTOR_COLUMNS, on_vector=True)
            cast(i, VECTOR_COLUMNS, P, on_vector=False)

        load_words(0)
        nc.sync.dma_start(offsets[:], offs)
        load_weights(0)
        load_scales()
        load_weights(1)
        load_weights(2)
        load_words(1)
        load_weights(5)
        load_weights(3)
        gather_words(0)
        gather_scales()
        load_weights(4)
        load_weights(5, starts=(P,))
        for c in range(TAPS):
            cast(c, 0, M, on_vector=False)
            quantize(c)
            multiply(c, (0, P))
            if c == 0:
                shift_words(0, c)
                shift_scales(0, c)
            if c == 1:
                gather_words(1)
            if c == 2:
                shift_words(1, c)
        cast(6, 0, P, on_vector=False)
        quantize(6)
        cast(3, 0, VECTOR_COLUMNS, on_vector=True)
        cast(3, VECTOR_COLUMNS, M, on_vector=False)
        shift_scales(1, 2)
        quantize(3)
        cast_shared(4)
        cast_shared(5)
        quantize(4)
        quantize(5)
        cast_shared(7)
        quantize(7)
        multiply(6, (0,))
        multiply(3, (0,))
        multiply(3, (P,))
        multiply(4, (0,), stop=True)
        multiply(5, (0,))
        multiply(7, (0,), stop=True)

        for t in range(M_TILES):
            for h in range(S // (2 * N)):
                result = keep.tile([P, 2 * N], F32, name=f"result{t}_{h}")
                if t == 1:
                    nc.scalar.activation(result[:, :N], acc[t][2 * h][:], ACT.Relu)
                    nc.vector.tensor_scalar_max(result[:, N:], acc[t][2 * h + 1][:], 0.0)
                else:
                    nc.scalar.activation(result[:], acc[t][h][:], ACT.Relu)
                nc.sync.dma_start(out[t * P : (t + 1) * P, 2 * h * N : 2 * (h + 1) * N], result[:])
